import numpy as np
import ml_dtypes


def mxq(x, axis, fmt="e4m3"):
    dtype, down = {"e4m3": (ml_dtypes.float8_e4m3fn, 7), "e5m2": (ml_dtypes.float8_e5m2, 14)}[fmt]
    v = np.moveaxis(np.asarray(x, np.float32).astype(ml_dtypes.bfloat16).astype(np.float64), axis, -1)
    blocks = v.reshape(v.shape[:-1] + (-1, 32))
    amax = np.abs(blocks).max(-1, keepdims=True)
    byte = np.maximum(np.where(amax > 0, np.frexp(amax)[1] - 1 + 127, 0) - down, 1)
    scale = np.exp2(byte - 127.0)
    codes = (blocks / scale).astype(np.float32).astype(dtype).astype(np.float64)
    return np.moveaxis((codes * scale).reshape(v.shape), -1, axis)


WIDE = False


def mx_kscale(k):
    if not WIDE:
        return np.ones(k)
    levels = np.array([10, -10, 5, -5, 0])
    if k % 512:
        return np.exp2(np.random.permutation(np.resize(levels, k // 32))).repeat(32)
    a = np.empty((k // 512, 16))
    for p in range(k // 512):
        a[p, :8] = np.random.permutation(np.resize(levels, 8))
        for g in range(8):
            far = levels[np.abs(levels - a[p, g]) >= 10]
            a[p, g + 8] = far[np.random.randint(len(far))]
    return np.exp2(a.ravel()).repeat(32)


def f64(x):
    return np.asarray(x).astype(np.float64)


def striped(idx):
    return np.tile(idx.reshape(-1, 16).T, (8, 1)).astype(np.uint16)


def unstriped(offs):
    return offs[:16].T.reshape(-1).astype(np.int64)


E2M1 = np.array([0.0, 0.5, 1.0, 1.5, 2.0, 3.0, 4.0, 6.0, -0.0, -0.5, -1.0, -1.5, -2.0, -3.0, -4.0, -6.0])


def pack_weight(w, fmt):
    k, n = w.shape
    w = f64(np.asarray(w, np.float32).astype(ml_dtypes.bfloat16)).reshape(k // 32, 32, n)
    amax = np.abs(w).max(1)
    if fmt == "e4m3":
        byte = np.frexp(amax)[1] - 1 + 127 - 7
    else:
        mant, ex = np.frexp(amax / 6.0)
        byte = np.where(mant > 0.5, ex, ex - 1) + 127
    byte = np.clip(np.where(amax > 0, byte, 1), 1, 254)
    scaled = (w * np.exp2(127.0 - byte)[:, None, :]).reshape(k, n).astype(np.float32)
    by_word = np.ascontiguousarray(scaled.reshape(k // 512, 128, 4, n).transpose(0, 1, 3, 2))
    if fmt == "e4m3":
        words = by_word.astype(ml_dtypes.float8_e4m3fn).view(np.uint8)
    else:
        c = by_word.astype(ml_dtypes.float4_e2m1fn).view(np.uint8) & 0xF
        words = (c[..., 0::2] | (c[..., 1::2] << 4)).reshape(k // 512, 128, 2 * n)
    return np.ascontiguousarray(words), np.ascontiguousarray(byte.astype(np.uint8).reshape(k // 512, 16, n))


def unpack_weight(words, scales, fmt):
    g, _, n = scales.shape
    words = np.ascontiguousarray(words).reshape(g, 128, n, -1)
    if fmt == "e4m3":
        vals = words.view(ml_dtypes.float8_e4m3fn).astype(np.float64)
    else:
        nib = np.empty((g, 128, n, 4), np.uint8)
        nib[..., 0::2] = words & 0xF
        nib[..., 1::2] = words >> 4
        vals = E2M1[nib]
    vals = vals * np.repeat(np.exp2(scales.astype(np.float64) - 127.0), 8, axis=1)[..., None]
    return vals.transpose(0, 1, 3, 2).reshape(g * 512, n)


def gelu(v):
    return 0.5 * v * (1.0 + np.tanh(np.sqrt(2.0 / np.pi) * (v + 0.044715 * v**3)))


def bf(x):
    return np.asarray(x, np.float32).astype(ml_dtypes.bfloat16)


def planes(Y):
    n, m = Y.shape
    b = f64(bf(Y)).reshape(n // 32, 32, m)
    amax = np.abs(b).max(1)
    byte = np.clip(np.where(amax > 0, np.frexp(amax)[1] - 1 + 127 - 7, 1), 1, 254)
    codes = (b * np.exp2(127.0 - byte)[:, None, :]).reshape(n, m).astype(np.float32).astype(ml_dtypes.float8_e4m3fn).view(np.uint8)
    words = codes.reshape(n // 512, 128, 4, m).transpose(0, 1, 3, 2)
    return np.ascontiguousarray(words), np.ascontiguousarray(byte.astype(np.uint8).reshape(n // 512, 16, m))


T, S, P, K, H, N = 4096, 1024, 512, 1024, 1536, 1024

def setup_inputs():
    n = np.random.standard_normal
    s = mx_kscale(K)[:, None]
    u = mx_kscale(H)[:, None]
    size = np.exp(0.8 * n(N))
    d = {}
    d["tab_words"], d["tab_scales"] = pack_weight(n((K, T)) * s, "e2m1")
    d["offs"] = striped(np.random.permutation(T)[:S])
    d["pos1"] = striped(np.random.permutation(S)[:P])
    d["pos2"] = striped(np.random.permutation(S)[:P])
    d["w1"] = (n((K, H)) / s / K**0.5).astype(np.float32)
    d["b1"] = (0.5 * n(H)).astype(np.float32)
    d["gain"] = (np.exp(0.3 * n(H)) * u[:, 0]).astype(np.float32)
    d["w2_words"], d["w2_scales"] = pack_weight(n((H, N)) * size[None, :] / u / H**0.5, "e2m1")
    d["sens"] = (0.8 * n((N, P)) * size[:, None]).astype(np.float32)
    return d

def reference(tab_words, tab_scales, offs, pos1, pos2, w1, b1, gain, w2_words, w2_scales, sens):
    v = unpack_weight(tab_words, tab_scales, "e2m1")[:, unstriped(offs)]
    a = (mxq(f64(w1), 0, "e4m3").T @ v) + f64(b1)[:, None]
    h = np.abs(a) * f64(gain)[:, None]
    x = np.maximum(h[:, unstriped(pos1)], h[:, unstriped(pos2)])
    z = mxq(x, 0, "e4m3")
    w2 = unpack_weight(w2_words, w2_scales, "e2m1")
    y = (w2.T @ z) + f64(sens)
    words, scales = planes(y)
    return y, words, scales

@@ -1,0 +1,264 @@
+from contextlib import ExitStack
+
+import concourse.mybir as mybir
+
+T, S, M, K, H, N = 4096, 1024, 512, 1024, 1536, 1024
+FLOPS = 2 * K * H * S + 2 * H * N * M
+
+F32 = mybir.dt.float32
+BF16 = mybir.dt.bfloat16
+I32 = mybir.dt.int32
+U32 = mybir.dt.uint32
+U16 = mybir.dt.uint16
+U8 = mybir.dt.uint8
+FP8X4 = mybir.dt.float8_e4m3fn_x4
+FP4X4 = mybir.dt.float4_e2m1fn_x4
+ALU = mybir.AluOpType
+ACT = mybir.ActivationFunctionType
+
+P = 128
+PACK = 4
+PASS = P * PACK
+BANK = 512
+K_PASSES = K // PASS
+H_PASSES = H // PASS
+N_GROUPS = N // PASS
+ROWS = 16
+
+
+def tile_list_banknote_plate_scores_kernel(
+    tc, tab_words, tab_scales, offs, pos1, pos2, w1, b1, gain, w2_words, w2_scales, sens, out_0, out_1, out_2
+):
+    nc = tc.nc
+    with ExitStack() as ctx:
+        lists = ctx.enter_context(tc.tile_pool(name="lists", bufs=1))
+        keep = ctx.enter_context(tc.tile_pool(name="keep", bufs=1))
+        psum = ctx.enter_context(tc.psum_pool(name="psum", bufs=1))
+
+        def bank(i, name):
+            return psum.tile([P, BANK], F32, tag="bank%d" % i, name=name)
+
+        def place_scale_rows(queue, planes, rows, passes):
+            for a in range(passes):
+                for q in range(4):
+                    queue.dma_start(
+                        out=planes[a][32 * q : 32 * q + 4, :].bitcast(I32),
+                        in_=rows[ROWS * a + 4 * q : ROWS * a + 4 * q + 4, :].bitcast(I32),
+                    )
+
+        warm = keep.tile([P, 2], F32, name="warm")
+        nc.gpsimd.memset(warm[:, 0:1], 0.0)
+        nc.scalar.activation(out=warm[:, 1:2], in_=warm[:, 0:1], func=ACT.Abs)
+
+        offs_t = lists.tile([P, S // 16], U16, name="offs_t")
+        pos1_t = lists.tile([P, M // 16], U16, name="pos1_t")
+        pos2_t = lists.tile([P, M // 16], U16, name="pos2_t")
+        nc.sync.dma_start(offs_t[:], offs)
+
+        tab_rows = keep.tile([P, T], U8, name="tab_rows", align_bytes=64)
+        nc.vector.memset(tab_rows[32:64, :].bitcast(I32), 0)
+        nc.vector.memset(tab_rows[64:128, :].bitcast(I32), 0)
+        nc.sync.dma_start(
+            out=tab_rows[0:32, :].bitcast(I32), in_=tab_scales.rearrange("a q c -> (a q) c").bitcast(I32)
+        )
+        v_planes = [keep.tile([P, S], U8, name="v_plane%d" % a, align_bytes=64) for a in range(K_PASSES)]
+        for plane in v_planes:
+            nc.vector.memset(plane[:].bitcast(I32), 0)
+
+        tabs = []
+        for a in range(K_PASSES):
+            if a == 0:
+                tab = keep.tile([P, T], U16, name="tab0", tag="raw", bufs=2, align_bytes=64)
+            else:
+                tab = keep.tile([P, T], U16, name="tab1", align_bytes=64)
+            nc.sync.dma_start(out=tab[:].bitcast(I32), in_=tab_words[a].bitcast(I32))
+            tabs.append(tab)
+        nc.sync.dma_start(pos1_t[:], pos1)
+        nc.sync.dma_start(pos2_t[:], pos2)
+
+        gain_t = keep.tile([P, H_PASSES, PACK], F32, name="gain_t")
+        b1_t = keep.tile([P, H_PASSES, PACK], F32, name="b1_t")
+        nc.gpsimd.dma_start(out=gain_t[:], in_=gain.rearrange("(b p t) -> p b t", p=P, t=PACK))
+        nc.gpsimd.dma_start(out=b1_t[:], in_=b1.rearrange("(b p t) -> p b t", p=P, t=PACK))
+        bias_t = keep.tile([P, H_PASSES, PACK], F32, name="bias_t")
+        nc.gpsimd.tensor_tensor(out=bias_t[:], in0=gain_t[:], in1=b1_t[:], op=ALU.mult)
+
+        def load_rows(name, rows):
+            raw = keep.tile([P, PACK, BANK], F32, name=name, tag="raw", bufs=2, align_bytes=64)
+            nc.sync.dma_start(out=raw[:], in_=rows.rearrange("(p j) c -> p j c", j=PACK))
+            return raw
+
+        def load_w1(b, a):
+            return load_rows("w1_%d%d" % (b, a), w1[PASS * a : PASS * (a + 1), PASS * b : PASS * (b + 1)])
+
+        def grouped_tile(name, tag):
+            return keep.tile([P, PACK * BANK], BF16, name=name, tag=tag, align_bytes=64)
+
+        def cast_w1(copy, grouped, raw, q0, q1):
+            copy(
+                out=grouped[:].rearrange("p (t q j) -> p q j t", t=PACK, j=PACK)[:, q0:q1],
+                in_=raw[:].rearrange("p j (q t) -> p q j t", t=PACK)[:, q0:q1],
+            )
+
+        def cast_whole(b, a):
+            raw = load_w1(b, a)
+            grouped = grouped_tile("w1g_%d%d" % (b, a), "grouped%d" % a)
+            cast_w1(nc.scalar.copy, grouped, raw, 0, P)
+            return grouped
+
+        def quantize(name, grouped, cuts=(0, BANK)):
+            codes = keep.tile([P, BANK], U32, name=name + "_codes", align_bytes=64)
+            scales = keep.tile([P, BANK], U8, name=name + "_scales", align_bytes=64)
+            for c0, c1 in zip(cuts, cuts[1:]):
+                nc.vector.quantize_mx(
+                    out=codes[:, c0:c1].bitcast(FP8X4), scales=scales[:, c0:c1], in_=grouped[:, PACK * c0 : PACK * c1]
+                )
+            return codes, scales
+
+        raw00 = load_w1(0, 0)
+
+        v_rows = keep.tile([P, S], U8, name="v_rows", align_bytes=64)
+        nc.vector.tensor_copy(out=v_rows[:], in_=tab_rows[:].indirect(offs_t[:]))
+        place_scale_rows(nc.scalar, v_planes, v_rows, K_PASSES)
+        v_words = []
+        for a in range(K_PASSES):
+            words = keep.tile([P, S], U16, name="v_words%d" % a, align_bytes=64)
+            nc.vector.tensor_copy(out=words[:], in_=tabs[a][:].indirect(offs_t[:]))
+            v_words.append(words)
+
+        raw01 = keep.tile([P, PACK, BANK], F32, name="w1_01", tag="raw", bufs=2, align_bytes=64)
+        rows01 = w1[PASS : 2 * PASS, 0:PASS].rearrange("(p j) c -> p j c", j=PACK)
+        for half in range(2):
+            cols = slice(256 * half, 256 * (half + 1))
+            nc.sync.dma_start(out=raw01[:, :, cols], in_=rows01[:, :, cols])
+
+        def first_stage(b, w1q):
+            tiles = []
+            for t in range(PACK):
+                h = keep.tile([P, S], F32, name="h_%d%d" % (b, t))
+                accs = [bank(2 * t + half, "acc_%d%d%d" % (b, t, half)) for half in range(S // BANK)]
+                for a in range(K_PASSES):
+                    codes, scales = w1q[a]
+                    for half, acc in enumerate(accs):
+                        cols = slice(BANK * half, BANK * (half + 1))
+                        nc.tensor.matmul_mx(
+                            out=acc[:],
+                            lhsT=codes[:, P * t : P * (t + 1)].bitcast(FP8X4),
+                            lhsT_scale=scales[:, P * t : P * (t + 1)],
+                            rhs=v_words[a][:, cols].bitcast(FP4X4),
+                            rhs_scale=v_planes[a][:, cols],
+                            start=(a == 0),
+                            stop=(a == K_PASSES - 1),
+                        )
+                for half, acc in enumerate(accs):
+                    nc.scalar.activation(
+                        out=h[:, BANK * half : BANK * (half + 1)],
+                        in_=acc[:],
+                        func=ACT.Abs,
+                        bias=bias_t[:, b, t : t + 1],
+                        scale=gain_t[:, b, t : t + 1],
+                    )
+                tiles.append(h)
+            return tiles
+
+        def pick(b, hs):
+            g1 = keep.tile([P, PACK, M], F32, name="g1_%d" % b, tag="g1")
+            g2 = keep.tile([P, PACK, M], F32, name="g2_%d" % b, tag="g2")
+            for t in range(PACK):
+                nc.vector.tensor_copy(out=g1[:, t, :], in_=hs[t][:].indirect(pos1_t[:]))
+                nc.vector.tensor_copy(out=g2[:, t, :], in_=hs[t][:].indirect(pos2_t[:]))
+            return g1, g2
+
+        def stronger(b, g1, g2):
+            grouped = grouped_tile("xg_%d" % b, "grouped1")
+            nc.vector.tensor_tensor(
+                out=grouped[:].rearrange("p (c i t) -> p c t i", i=2, t=PACK),
+                in0=g1[:].rearrange("p t (c i) -> p c t i", i=2),
+                in1=g2[:].rearrange("p t (c i) -> p c t i", i=2),
+                op=ALU.max,
+            )
+            return quantize("x%d" % b, grouped)
+
+        def deal_w2_words():
+            w2_raw = keep.tile([P, H_PASSES, N], U16, name="w2_raw", tag="raw", bufs=2, align_bytes=64)
+            nc.sync.dma_start(out=w2_raw[:].bitcast(I32), in_=w2_words.rearrange("a p c -> p a c").bitcast(I32))
+            w2_dealt = keep.tile([P, H_PASSES * N], U16, name="w2_dealt", align_bytes=64)
+            nc.vector.tensor_copy(
+                out=w2_dealt[:].rearrange("p (g t q) -> p g t q", t=PACK, q=P),
+                in_=w2_raw[:].rearrange("p a (g q t) -> p (a g) t q", t=PACK, q=P),
+            )
+            return w2_dealt
+
+        def deal_w2_scales():
+            w2_rows = keep.tile([P, N], U8, name="w2_rows", align_bytes=64)
+            nc.gpsimd.memset(w2_rows[:].bitcast(I32), 0)
+            nc.gpsimd.dma_start(
+                out=w2_rows[0 : ROWS * H_PASSES, :].bitcast(I32),
+                in_=w2_scales.rearrange("a q c -> (a q) c").bitcast(I32),
+            )
+            rows_dealt = keep.tile([P, N], U8, name="w2_rows_dealt", tag="grouped0", align_bytes=64)
+            nc.vector.tensor_copy(
+                out=rows_dealt[:].rearrange("p (g t q) -> p g t q", t=PACK, q=P),
+                in_=w2_rows[:].rearrange("p (g q t) -> p g t q", t=PACK, q=P),
+            )
+            w2_planes = [keep.tile([P, N], U8, name="w2_plane%d" % a, align_bytes=64) for a in range(H_PASSES)]
+            for plane in w2_planes:
+                nc.gpsimd.memset(plane[:].bitcast(I32), 0)
+            place_scale_rows(nc.sync, w2_planes, rows_dealt, H_PASSES)
+            return w2_planes
+
+        grouped00 = grouped_tile("w1g_00", "grouped0")
+        cast_w1(nc.scalar.copy, grouped00, raw00, 0, 80)
+        cast_w1(nc.vector.tensor_copy, grouped00, raw00, 80, P)
+        q00 = quantize("w1_00", grouped00)
+        grouped01 = grouped_tile("w1g_01", "grouped1")
+        cast_w1(nc.scalar.copy, grouped01, raw01, 0, 64)
+        cast_w1(nc.vector.tensor_copy, grouped01, raw01, 64, P)
+        w1q = [q00, quantize("w1_01", grouped01, (0, 128, 256, 512))]
+        w2_dealt = deal_w2_words()
+        hs = first_stage(0, w1q)
+        xq = []
+        for b in range(H_PASSES):
+            g1, g2 = pick(b, hs)
+            if b + 1 < H_PASSES:
+                w1q = [quantize("w1_%d%d" % (b + 1, a), cast_whole(b + 1, a)) for a in range(K_PASSES)]
+                hs = first_stage(b + 1, w1q)
+            if b == 1:
+                w2_planes = deal_w2_scales()
+                sens_t = [load_rows("sens%d" % g, sens[PASS * g : PASS * (g + 1), :]) for g in range(N_GROUPS)]
+            xq.append(stronger(b, g1, g2))
+
+        accs = [bank(i, "score%d" % i) for i in range(N // P)]
+        for b in range(H_PASSES):
+            codes, scales = xq[b]
+            for i, acc in enumerate(accs):
+                nc.tensor.matmul_mx(
+                    out=acc[:],
+                    lhsT=w2_dealt[:, N * b + P * i : N * b + P * (i + 1)].bitcast(FP4X4),
+                    lhsT_scale=w2_planes[b][:, P * i : P * (i + 1)],
+                    rhs=codes[:].bitcast(FP8X4),
+                    rhs_scale=scales[:],
+                    start=(b == 0),
+                    stop=(b == H_PASSES - 1),
+                )
+        for g in range(N_GROUPS):
+            y = keep.tile([P, PACK, M], F32, name="y%d" % g)
+            rows = out_0[PASS * g : PASS * (g + 1), :].rearrange("(p t) m -> p t m", t=PACK)
+            for t in range(PACK):
+                nc.vector.tensor_tensor(out=y[:, t, :], in0=accs[PACK * g + t][:], in1=sens_t[g][:, t, :], op=ALU.add)
+                nc.sync.dma_start(out=rows[:, t, :], in_=y[:, t, :])
+            grouped = keep.tile([P, PACK * M], BF16, name="yg%d" % g, align_bytes=64)
+            woven = grouped[:].rearrange("p (c i t) -> p c t i", i=4, t=PACK)
+            planar = y[:].rearrange("p t (c i) -> p c t i", i=4)
+            cut = M // 4 if g == 0 else 36
+            nc.scalar.copy(out=woven[:, :cut], in_=planar[:, :cut])
+            if cut < M // 4:
+                nc.vector.tensor_copy(out=woven[:, cut:], in_=planar[:, cut:])
+            codes, scales = quantize("y%d" % g, grouped)
+            nc.sync.dma_start(
+                out=out_1[g].rearrange("p m t -> p (m t)").bitcast(I32), in_=codes[:].bitcast(I32)
+            )
+            for q in range(4):
+                nc.scalar.dma_start(
+                    out=out_2[g, 4 * q : 4 * q + 4, :].bitcast(I32), in_=scales[32 * q : 32 * q + 4, :].bitcast(I32)
+                )

@@ -1,6 +1,7 @@
 from contextlib import ExitStack
 
 import concourse.mybir as mybir
+from concourse.masks import make_identity
 
 T, S, M, K, H, N = 4096, 1024, 512, 1024, 1536, 1024
 FLOPS = 2 * K * H * S + 2 * H * N * M
@@ -38,13 +39,12 @@ def tile_list_banknote_plate_scores_kernel(
         def bank(i, name):
             return psum.tile([P, BANK], F32, tag="bank%d" % i, name=name)
 
-        def place_scale_rows(queue, planes, rows, passes):
-            for a in range(passes):
-                for q in range(4):
-                    queue.dma_start(
-                        out=planes[a][32 * q : 32 * q + 4, :].bitcast(I32),
-                        in_=rows[ROWS * a + 4 * q : ROWS * a + 4 * q + 4, :].bitcast(I32),
-                    )
+        def place_scale_rows(planes, rows, first, last):
+            for i in range(first, last):
+                a, q = divmod(i, 4)
+                nc.sync.dma_start(
+                    out=planes[a][32 * q : 32 * q + 4, :].bitcast(I32), in_=rows[4 * i : 4 * i + 4, :].bitcast(I32)
+                )
 
         warm = keep.tile([P, 2], F32, name="warm")
         nc.gpsimd.memset(warm[:, 0:1], 0.0)
@@ -94,17 +94,11 @@ def tile_list_banknote_plate_scores_kernel(
         def grouped_tile(name, tag):
             return keep.tile([P, PACK * BANK], BF16, name=name, tag=tag, align_bytes=64)
 
-        def cast_w1(copy, grouped, raw, q0, q1):
+        def cast_w1(copy, grouped, raw, q0, q1, t0=0, t1=PACK):
             copy(
-                out=grouped[:].rearrange("p (t q j) -> p q j t", t=PACK, j=PACK)[:, q0:q1],
-                in_=raw[:].rearrange("p j (q t) -> p q j t", t=PACK)[:, q0:q1],
+                out=grouped[:].rearrange("p (t q j) -> p q j t", t=PACK, j=PACK)[:, q0:q1, :, t0:t1],
+                in_=raw[:].rearrange("p j (q t) -> p q j t", t=PACK)[:, q0:q1, :, t0:t1],
             )
-
-        def cast_whole(b, a):
-            raw = load_w1(b, a)
-            grouped = grouped_tile("w1g_%d%d" % (b, a), "grouped%d" % a)
-            cast_w1(nc.scalar.copy, grouped, raw, 0, P)
-            return grouped
 
         def quantize(name, grouped, cuts=(0, BANK)):
             codes = keep.tile([P, BANK], U32, name=name + "_codes", align_bytes=64)
@@ -119,7 +113,7 @@ def tile_list_banknote_plate_scores_kernel(
 
         v_rows = keep.tile([P, S], U8, name="v_rows", align_bytes=64)
         nc.vector.tensor_copy(out=v_rows[:], in_=tab_rows[:].indirect(offs_t[:]))
-        place_scale_rows(nc.scalar, v_planes, v_rows, K_PASSES)
+        place_scale_rows(v_planes, v_rows, 0, 5)
         v_words = []
         for a in range(K_PASSES):
             words = keep.tile([P, S], U16, name="v_words%d" % a, align_bytes=64)
@@ -131,20 +125,21 @@ def tile_list_banknote_plate_scores_kernel(
         for half in range(2):
             cols = slice(256 * half, 256 * (half + 1))
             nc.sync.dma_start(out=raw01[:, :, cols], in_=rows01[:, :, cols])
+        place_scale_rows(v_planes, v_rows, 5, 4 * K_PASSES)
 
-        def first_stage(b, w1q):
+        def first_stage(b, stationary):
             tiles = []
             for t in range(PACK):
-                h = keep.tile([P, S], F32, name="h_%d%d" % (b, t))
-                accs = [bank(2 * t + half, "acc_%d%d%d" % (b, t, half)) for half in range(S // BANK)]
+                h = keep.tile([P, S], F32, name="h_%d%d" % (b, t), tag="h_%d%d" % (b, t), align_bytes=64)
+                accs = [bank(2 * (t % 2) + half, "acc_%d%d%d" % (b, t, half)) for half in range(S // BANK)]
                 for a in range(K_PASSES):
-                    codes, scales = w1q[a]
+                    codes, scales = stationary(t, a)
                     for half, acc in enumerate(accs):
                         cols = slice(BANK * half, BANK * (half + 1))
                         nc.tensor.matmul_mx(
                             out=acc[:],
-                            lhsT=codes[:, P * t : P * (t + 1)].bitcast(FP8X4),
-                            lhsT_scale=scales[:, P * t : P * (t + 1)],
+                            lhsT=codes.bitcast(FP8X4),
+                            lhsT_scale=scales,
                             rhs=v_words[a][:, cols].bitcast(FP4X4),
                             rhs_scale=v_planes[a][:, cols],
                             start=(a == 0),
@@ -161,104 +156,217 @@ def tile_list_banknote_plate_scores_kernel(
                 tiles.append(h)
             return tiles
 
-        def pick(b, hs):
-            g1 = keep.tile([P, PACK, M], F32, name="g1_%d" % b, tag="g1")
-            g2 = keep.tile([P, PACK, M], F32, name="g2_%d" % b, tag="g2")
+        def pick(b, hs, m0, m1, tag):
+            g1 = keep.tile([P, PACK, m1 - m0], F32, name="g1_%d_%d" % (b, m0), tag=tag + "1")
+            g2 = keep.tile([P, PACK, m1 - m0], F32, name="g2_%d_%d" % (b, m0), tag=tag + "2")
             for t in range(PACK):
-                nc.vector.tensor_copy(out=g1[:, t, :], in_=hs[t][:].indirect(pos1_t[:]))
-                nc.vector.tensor_copy(out=g2[:, t, :], in_=hs[t][:].indirect(pos2_t[:]))
+                nc.vector.tensor_copy(out=g1[:, t, :], in_=hs[t][:].indirect(pos1_t[:, m0 // 16 : m1 // 16]))
+                nc.vector.tensor_copy(out=g2[:, t, :], in_=hs[t][:].indirect(pos2_t[:, m0 // 16 : m1 // 16]))
             return g1, g2
 
-        def stronger(b, g1, g2):
-            grouped = grouped_tile("xg_%d" % b, "grouped1")
+        def stronger(grouped, g1, g2):
             nc.vector.tensor_tensor(
-                out=grouped[:].rearrange("p (c i t) -> p c t i", i=2, t=PACK),
+                out=grouped.rearrange("p (c i t) -> p c t i", i=2, t=PACK),
                 in0=g1[:].rearrange("p t (c i) -> p c t i", i=2),
                 in1=g2[:].rearrange("p t (c i) -> p c t i", i=2),
                 op=ALU.max,
             )
-            return quantize("x%d" % b, grouped)
 
-        def deal_w2_words():
-            w2_raw = keep.tile([P, H_PASSES, N], U16, name="w2_raw", tag="raw", bufs=2, align_bytes=64)
-            nc.sync.dma_start(out=w2_raw[:].bitcast(I32), in_=w2_words.rearrange("a p c -> p a c").bitcast(I32))
-            w2_dealt = keep.tile([P, H_PASSES * N], U16, name="w2_dealt", align_bytes=64)
-            nc.vector.tensor_copy(
-                out=w2_dealt[:].rearrange("p (g t q) -> p g t q", t=PACK, q=P),
-                in_=w2_raw[:].rearrange("p a (g q t) -> p (a g) t q", t=PACK, q=P),
-            )
-            return w2_dealt
+        def mx_tiles(name, shape):
+            codes = keep.tile(shape, U32, name=name + "_codes", align_bytes=64)
+            scales = keep.tile(shape, U8, name=name + "_scales", align_bytes=64)
+            return codes, scales
 
-        def deal_w2_scales():
-            w2_rows = keep.tile([P, N], U8, name="w2_rows", align_bytes=64)
-            nc.gpsimd.memset(w2_rows[:].bitcast(I32), 0)
-            nc.gpsimd.dma_start(
-                out=w2_rows[0 : ROWS * H_PASSES, :].bitcast(I32),
-                in_=w2_scales.rearrange("a q c -> (a q) c").bitcast(I32),
+        def turn_sens(j0, j1):
+            turned = []
+            for j in range(j0, j1):
+                st = keep.tile([P, N_GROUPS, PACK, P], F32, name="sens_turned%d" % j)
+                for g in range(N_GROUPS):
+                    acc = bank(4 + (N_GROUPS * j + g) % 4, "sens_acc%d%d" % (j, g))
+                    for t in range(PACK):
+                        nc.tensor.transpose(acc[:, P * t : P * (t + 1)], sens_t[g][:, t, P * j : P * (j + 1)], ident[:])
+                    nc.scalar.copy(out=st[:, g].rearrange("p t q -> p (t q)"), in_=acc[:])
+                turned.append(st)
+            return turned
+
+        def load_w2_scales():
+            planes = keep.tile([P, H_PASSES, N], U8, name="w2_planes", tag="h_03", align_bytes=64)
+            nc.gpsimd.memset(planes[:].rearrange("p a c -> p (a c)").bitcast(I32), 0)
+            for q in range(4):
+                nc.sync.dma_start(
+                    out=planes[32 * q : 32 * q + 4].bitcast(I32),
+                    in_=w2_scales[:, 4 * q : 4 * q + 4, :].rearrange("a r c -> r a c").bitcast(I32),
+                )
+            return planes
+
+        def load_sens(g, tag):
+            rows = keep.tile([P, PACK, M], F32, name="sens%d" % g, tag=tag, align_bytes=64)
+            nc.sync.dma_start(out=rows[:], in_=sens[PASS * g : PASS * (g + 1), :].rearrange("(p t) m -> p t m", t=PACK))
+            return rows
+
+        def quantize_into(tiles, grouped, c0, c1):
+            codes, scales = tiles
+            nc.vector.quantize_mx(
+                out=codes[:, c0:c1].bitcast(FP8X4), scales=scales[:, c0:c1], in_=grouped[:, PACK * c0 : PACK * c1]
             )
-            rows_dealt = keep.tile([P, N], U8, name="w2_rows_dealt", tag="grouped0", align_bytes=64)
-            nc.vector.tensor_copy(
-                out=rows_dealt[:].rearrange("p (g t q) -> p g t q", t=PACK, q=P),
-                in_=w2_rows[:].rearrange("p (g q t) -> p g t q", t=PACK, q=P),
-            )
-            w2_planes = [keep.tile([P, N], U8, name="w2_plane%d" % a, align_bytes=64) for a in range(H_PASSES)]
-            for plane in w2_planes:
-                nc.gpsimd.memset(plane[:].bitcast(I32), 0)
-            place_scale_rows(nc.sync, w2_planes, rows_dealt, H_PASSES)
-            return w2_planes
+
+        def later_weights(b):
+            grouped = keep.tile([P, K_PASSES * PACK * BANK], BF16, name="w1g_%d" % b, tag="weights%d" % b, align_bytes=64)
+            dealt = grouped[:].rearrange("p (t a q j) -> p a q j t", t=PACK, a=K_PASSES, j=PACK)
+            for a in range(K_PASSES):
+                raw = load_w1(b, a)
+                nc.scalar.copy(out=dealt[:, a], in_=raw[:].rearrange("p j (q t) -> p q j t", t=PACK))
+            tiles = mx_tiles("w1_%d" % b, [P, K_PASSES * BANK])
+            for c0, c1 in ((0, 256), (256, 512), (512, 1024)):
+                quantize_into(tiles, grouped, c0, c1)
+
+            def columns(t, a):
+                cols = slice(P * (K_PASSES * t + a), P * (K_PASSES * t + a + 1))
+                return tiles[0][:, cols], tiles[1][:, cols]
+
+            return columns
 
         grouped00 = grouped_tile("w1g_00", "grouped0")
-        cast_w1(nc.scalar.copy, grouped00, raw00, 0, 80)
-        cast_w1(nc.vector.tensor_copy, grouped00, raw00, 80, P)
-        q00 = quantize("w1_00", grouped00)
         grouped01 = grouped_tile("w1g_01", "grouped1")
-        cast_w1(nc.scalar.copy, grouped01, raw01, 0, 64)
-        cast_w1(nc.vector.tensor_copy, grouped01, raw01, 64, P)
-        w1q = [q00, quantize("w1_01", grouped01, (0, 128, 256, 512))]
-        w2_dealt = deal_w2_words()
-        hs = first_stage(0, w1q)
+        w1q = [mx_tiles("w1_0%d" % a, [P, BANK]) for a in range(K_PASSES)]
+        cast_w1(nc.scalar.copy, grouped00, raw00, 0, P, 0, 1)
+        quantize_into(w1q[0], grouped00, 0, P)
+        for half in range(2):
+            cast_w1(nc.vector.tensor_copy, grouped01, raw01, 64 * half, 64 * (half + 1), 0, 1)
+        quantize_into(w1q[1], grouped01, 0, P)
+        cast_w1(nc.scalar.copy, grouped00, raw00, 0, P, 1, PACK)
+        cast_w1(nc.scalar.copy, grouped01, raw01, 0, 64, 1, PACK)
+        cast_w1(nc.vector.tensor_copy, grouped01, raw01, 64, P, 1, PACK)
+        for a, grouped in enumerate((grouped00, grouped01)):
+            quantize_into(w1q[a], grouped, P, 2 * P)
+            quantize_into(w1q[a], grouped, 2 * P, BANK)
+        stationary = lambda t, a: (w1q[a][0][:, P * t : P * (t + 1)], w1q[a][1][:, P * t : P * (t + 1)])
+        ident = keep.tile([P, P], F32, name="ident")
+        make_identity(nc, ident[:])
+        hs = first_stage(0, stationary)
         xq = []
-        for b in range(H_PASSES):
-            g1, g2 = pick(b, hs)
-            if b + 1 < H_PASSES:
-                w1q = [quantize("w1_%d%d" % (b + 1, a), cast_whole(b + 1, a)) for a in range(K_PASSES)]
-                hs = first_stage(b + 1, w1q)
+        for b in range(H_PASSES - 1):
+            g1, g2 = pick(b, hs, 0, M, "g")
+            stationary = later_weights(b + 1)
             if b == 1:
-                w2_planes = deal_w2_scales()
-                sens_t = [load_rows("sens%d" % g, sens[PASS * g : PASS * (g + 1), :]) for g in range(N_GROUPS)]
-            xq.append(stronger(b, g1, g2))
+                sens_turned = turn_sens(0, 2)
+            hs = first_stage(b + 1, stationary)
+            if b == 1:
+                sens_turned = sens_turned + turn_sens(2, 4)
+            if b == 0:
+                sens_t = [load_sens(g, "h_0%d" % (2 * g)) for g in range(N_GROUPS)]
+                w2_t = keep.tile([P, H_PASSES, N], U16, name="w2_t", tag="h_01", align_bytes=64)
+                nc.sync.dma_start(out=w2_t[:].bitcast(I32), in_=w2_words.rearrange("a p c -> p a c").bitcast(I32))
+                w2_planes = load_w2_scales()
+            grouped = grouped_tile("xg_%d" % b, "weights%d" % (b + 1))
+            stronger(grouped[:], g1, g2)
+            xq.append(quantize("x%d" % b, grouped))
 
-        accs = [bank(i, "score%d" % i) for i in range(N // P)]
-        for b in range(H_PASSES):
-            codes, scales = xq[b]
-            for i, acc in enumerate(accs):
-                nc.tensor.matmul_mx(
-                    out=acc[:],
-                    lhsT=w2_dealt[:, N * b + P * i : N * b + P * (i + 1)].bitcast(FP4X4),
-                    lhsT_scale=w2_planes[b][:, P * i : P * (i + 1)],
-                    rhs=codes[:].bitcast(FP8X4),
-                    rhs_scale=scales[:],
-                    start=(b == 0),
-                    stop=(b == H_PASSES - 1),
+        last = H_PASSES - 1
+        x_codes, x_scales = mx_tiles("x_last", [P, M])
+        xq.append((x_codes, x_scales))
+        y_codes, y_scales = mx_tiles("y", [P, N_GROUPS, M])
+        ys = [keep.tile([P, PACK, M], F32, name="y%d" % g) for g in range(N_GROUPS)]
+
+        def sums_out(j, add_here):
+            m = slice(P * j, P * (j + 1))
+            sums = [bank(2 * (j % 2) + g, "sum%d%d" % (j, g)) for g in range(N_GROUPS)]
+            for b in range(H_PASSES):
+                codes, scales = xq[b]
+                for g in range(N_GROUPS):
+                    n = slice(PASS * g, PASS * (g + 1))
+                    nc.tensor.matmul_mx(
+                        out=sums[g][:],
+                        lhsT=codes[:, m].bitcast(FP8X4),
+                        lhsT_scale=scales[:, m],
+                        rhs=w2_t[:, b, n].bitcast(FP4X4),
+                        rhs_scale=w2_planes[:, b, n],
+                        start=(b == 0),
+                        stop=(b == H_PASSES - 1),
+                    )
+            zs = []
+            for g in range(N_GROUPS):
+                z = keep.tile([P, PACK, P], F32, name="z%d%d" % (j, g), tag="z%d" % g, bufs=2)
+                dealt = sums[g][:].rearrange("p (q t) -> p t q", t=PACK)
+                if add_here:
+                    nc.vector.tensor_tensor(out=z[:], in0=dealt, in1=sens_turned[j][:, g], op=ALU.add)
+                else:
+                    nc.scalar.copy(out=z[:], in_=dealt)
+                zs.append(z)
+            return zs
+
+        def turn_back(j, zs, add_here=True):
+            outs = []
+            for g in range(N_GROUPS):
+                acc = bank(4 + 2 * (j % 2) + g, "y_acc%d%d" % (j, g))
+                sources = (sens_turned[j][:, g], zs[g][:]) if add_here else (zs[g][:],)
+                for i, source in enumerate(sources):
+                    for t in range(PACK):
+                        nc.tensor.matmul(
+                            out=acc[:, P * t : P * (t + 1)],
+                            lhsT=source[:, t, :],
+                            rhs=ident[:],
+                            is_transpose=True,
+                            start=(i == 0 and t == 0),
+                            stop=(i == len(sources) - 1 and t == PACK - 1),
+                        )
+                outs.append(acc)
+            return outs
+
+        def make_planes(j, outs, copies):
+            m = slice(P * j, P * (j + 1))
+            for g in range(N_GROUPS):
+                woven = keep.tile([P, PACK * P], BF16, name="yg%d%d" % (j, g), tag="yg%d%d" % (j, g), align_bytes=64)
+                copies[g](
+                    out=woven[:].rearrange("p (m t) -> p m t", t=PACK),
+                    in_=outs[g][:].rearrange("p (t m) -> p m t", t=PACK),
                 )
-        for g in range(N_GROUPS):
-            y = keep.tile([P, PACK, M], F32, name="y%d" % g)
-            rows = out_0[PASS * g : PASS * (g + 1), :].rearrange("(p t) m -> p t m", t=PACK)
-            for t in range(PACK):
-                nc.vector.tensor_tensor(out=y[:, t, :], in0=accs[PACK * g + t][:], in1=sens_t[g][:, t, :], op=ALU.add)
-                nc.sync.dma_start(out=rows[:, t, :], in_=y[:, t, :])
-            grouped = keep.tile([P, PACK * M], BF16, name="yg%d" % g, align_bytes=64)
-            woven = grouped[:].rearrange("p (c i t) -> p c t i", i=4, t=PACK)
-            planar = y[:].rearrange("p t (c i) -> p c t i", i=4)
-            cut = M // 4 if g == 0 else 36
-            nc.scalar.copy(out=woven[:, :cut], in_=planar[:, :cut])
-            if cut < M // 4:
-                nc.vector.tensor_copy(out=woven[:, cut:], in_=planar[:, cut:])
-            codes, scales = quantize("y%d" % g, grouped)
+                nc.vector.quantize_mx(out=y_codes[:, g, m].bitcast(FP8X4), scales=y_scales[:, g, m], in_=woven[:])
+
+        def keep_scores(j, outs, copies):
+            for g in range(N_GROUPS):
+                copies[g](out=ys[g][:, :, P * j : P * (j + 1)], in_=outs[g][:].rearrange("p (t m) -> p t m", t=PACK))
+
+        def store(m0, m1):
+            for g in range(N_GROUPS):
+                rows = out_0[PASS * g : PASS * (g + 1), :].rearrange("(p t) m -> p t m", t=PACK)
+                nc.sync.dma_start(out=rows[:, :, m0:m1], in_=ys[g][:, :, m0:m1])
             nc.sync.dma_start(
-                out=out_1[g].rearrange("p m t -> p (m t)").bitcast(I32), in_=codes[:].bitcast(I32)
+                out=out_1[:, :, m0:m1, :].rearrange("g p m t -> p g (m t)").bitcast(I32),
+                in_=y_codes[:, :, m0:m1].bitcast(I32),
             )
-            for q in range(4):
-                nc.scalar.dma_start(
-                    out=out_2[g, 4 * q : 4 * q + 4, :].bitcast(I32), in_=scales[32 * q : 32 * q + 4, :].bitcast(I32)
-                )
+
+        def last_block(m0, m1, tag, grouped_tag):
+            g1, g2 = pick(last, hs, m0, m1, tag)
+            grouped = keep.tile([P, PACK * (m1 - m0)], BF16, name="xg_last%d" % m0, tag=grouped_tag, align_bytes=64)
+            stronger(grouped[:], g1, g2)
+            nc.vector.quantize_mx(out=x_codes[:, m0:m1].bitcast(FP8X4), scales=x_scales[:, m0:m1], in_=grouped[:])
+
+        on_scalar = (nc.scalar.copy, nc.scalar.copy)
+        shared = (nc.vector.tensor_copy, nc.scalar.copy)
+        last_block(0, 256, "g", "xg_a")
+        zs = [sums_out(j, False) for j in range(2)]
+        outs0 = turn_back(0, zs[0])
+        make_planes(0, outs0, on_scalar)
+        keep_scores(0, outs0, on_scalar)
+        outs1 = turn_back(1, zs[1])
+        make_planes(1, outs1, on_scalar)
+        last_block(256, 384, "g", "xg_b")
+        zs2 = sums_out(2, False)
+        keep_scores(1, outs1, on_scalar)
+        store(0, 256)
+        outs2 = turn_back(2, zs2)
+        make_planes(2, outs2, on_scalar)
+        keep_scores(2, outs2, on_scalar)
+        store(256, 384)
+        last_block(384, 512, "g", "yg11")
+        outs3 = turn_back(3, sums_out(3, True), False)
+        make_planes(3, outs3, shared)
+        keep_scores(3, outs3, shared)
+        store(384, 512)
+        for q in range(4):
+            queue = nc.scalar if q % 2 else nc.sync
+            queue.dma_start(
+                out=out_2[:, 4 * q : 4 * q + 4, :].rearrange("g r m -> r g m").bitcast(I32),
+                in_=y_scales[32 * q : 32 * q + 4].bitcast(I32),
+            )

@@ -46,10 +46,6 @@ def tile_list_banknote_plate_scores_kernel(
                     out=planes[a][32 * q : 32 * q + 4, :].bitcast(I32), in_=rows[4 * i : 4 * i + 4, :].bitcast(I32)
                 )
 
-        warm = keep.tile([P, 2], F32, name="warm")
-        nc.gpsimd.memset(warm[:, 0:1], 0.0)
-        nc.scalar.activation(out=warm[:, 1:2], in_=warm[:, 0:1], func=ACT.Abs)
-
         offs_t = lists.tile([P, S // 16], U16, name="offs_t")
         pos1_t = lists.tile([P, M // 16], U16, name="pos1_t")
         pos2_t = lists.tile([P, M // 16], U16, name="pos2_t")

from contextlib import ExitStack

import concourse.mybir as mybir
from concourse.masks import make_identity

T, S, M, K, H, N = 4096, 1024, 512, 1024, 1536, 1024
FLOPS = 2 * K * H * S + 2 * H * N * M

F32 = mybir.dt.float32
BF16 = mybir.dt.bfloat16
I32 = mybir.dt.int32
U32 = mybir.dt.uint32
U16 = mybir.dt.uint16
U8 = mybir.dt.uint8
FP8X4 = mybir.dt.float8_e4m3fn_x4
FP4X4 = mybir.dt.float4_e2m1fn_x4
ALU = mybir.AluOpType
ACT = mybir.ActivationFunctionType

P = 128
PACK = 4
PASS = P * PACK
BANK = 512
K_PASSES = K // PASS
H_PASSES = H // PASS
N_GROUPS = N // PASS
ROWS = 16


def tile_list_banknote_plate_scores_kernel(
    tc, tab_words, tab_scales, offs, pos1, pos2, w1, b1, gain, w2_words, w2_scales, sens, out_0, out_1, out_2
):
    nc = tc.nc
    with ExitStack() as ctx:
        lists = ctx.enter_context(tc.tile_pool(name="lists", bufs=1))
        keep = ctx.enter_context(tc.tile_pool(name="keep", bufs=1))
        psum = ctx.enter_context(tc.psum_pool(name="psum", bufs=1))

        def bank(i, name):
            return psum.tile([P, BANK], F32, tag="bank%d" % i, name=name)

        def place_scale_rows(planes, rows, first, last):
            for i in range(first, last):
                a, q = divmod(i, 4)
                nc.sync.dma_start(
                    out=planes[a][32 * q : 32 * q + 4, :].bitcast(I32), in_=rows[4 * i : 4 * i + 4, :].bitcast(I32)
                )

        offs_t = lists.tile([P, S // 16], U16, name="offs_t")
        pos1_t = lists.tile([P, M // 16], U16, name="pos1_t")
        pos2_t = lists.tile([P, M // 16], U16, name="pos2_t")
        nc.sync.dma_start(offs_t[:], offs)

        tab_rows = keep.tile([P, T], U8, name="tab_rows", align_bytes=64)
        nc.vector.memset(tab_rows[32:64, :].bitcast(I32), 0)
        nc.vector.memset(tab_rows[64:128, :].bitcast(I32), 0)
        nc.sync.dma_start(
            out=tab_rows[0:32, :].bitcast(I32), in_=tab_scales.rearrange("a q c -> (a q) c").bitcast(I32)
        )
        v_planes = [keep.tile([P, S], U8, name="v_plane%d" % a, align_bytes=64) for a in range(K_PASSES)]
        for plane in v_planes:
            nc.vector.memset(plane[:].bitcast(I32), 0)

        tabs = []
        for a in range(K_PASSES):
            if a == 0:
                tab = keep.tile([P, T], U16, name="tab0", tag="raw", bufs=2, align_bytes=64)
            else:
                tab = keep.tile([P, T], U16, name="tab1", align_bytes=64)
            nc.sync.dma_start(out=tab[:].bitcast(I32), in_=tab_words[a].bitcast(I32))
            tabs.append(tab)
        nc.sync.dma_start(pos1_t[:], pos1)
        nc.sync.dma_start(pos2_t[:], pos2)

        gain_t = keep.tile([P, H_PASSES, PACK], F32, name="gain_t")
        b1_t = keep.tile([P, H_PASSES, PACK], F32, name="b1_t")
        nc.gpsimd.dma_start(out=gain_t[:], in_=gain.rearrange("(b p t) -> p b t", p=P, t=PACK))
        nc.gpsimd.dma_start(out=b1_t[:], in_=b1.rearrange("(b p t) -> p b t", p=P, t=PACK))
        bias_t = keep.tile([P, H_PASSES, PACK], F32, name="bias_t")
        nc.gpsimd.tensor_tensor(out=bias_t[:], in0=gain_t[:], in1=b1_t[:], op=ALU.mult)

        def load_rows(name, rows):
            raw = keep.tile([P, PACK, BANK], F32, name=name, tag="raw", bufs=2, align_bytes=64)
            nc.sync.dma_start(out=raw[:], in_=rows.rearrange("(p j) c -> p j c", j=PACK))
            return raw

        def load_w1(b, a):
            return load_rows("w1_%d%d" % (b, a), w1[PASS * a : PASS * (a + 1), PASS * b : PASS * (b + 1)])

        def grouped_tile(name, tag):
            return keep.tile([P, PACK * BANK], BF16, name=name, tag=tag, align_bytes=64)

        def cast_w1(copy, grouped, raw, q0, q1, t0=0, t1=PACK):
            copy(
                out=grouped[:].rearrange("p (t q j) -> p q j t", t=PACK, j=PACK)[:, q0:q1, :, t0:t1],
                in_=raw[:].rearrange("p j (q t) -> p q j t", t=PACK)[:, q0:q1, :, t0:t1],
            )

        def quantize(name, grouped, cuts=(0, BANK)):
            codes = keep.tile([P, BANK], U32, name=name + "_codes", align_bytes=64)
            scales = keep.tile([P, BANK], U8, name=name + "_scales", align_bytes=64)
            for c0, c1 in zip(cuts, cuts[1:]):
                nc.vector.quantize_mx(
                    out=codes[:, c0:c1].bitcast(FP8X4), scales=scales[:, c0:c1], in_=grouped[:, PACK * c0 : PACK * c1]
                )
            return codes, scales

        raw00 = load_w1(0, 0)

        v_rows = keep.tile([P, S], U8, name="v_rows", align_bytes=64)
        nc.vector.tensor_copy(out=v_rows[:], in_=tab_rows[:].indirect(offs_t[:]))
        place_scale_rows(v_planes, v_rows, 0, 5)
        v_words = []
        for a in range(K_PASSES):
            words = keep.tile([P, S], U16, name="v_words%d" % a, align_bytes=64)
            nc.vector.tensor_copy(out=words[:], in_=tabs[a][:].indirect(offs_t[:]))
            v_words.append(words)

        raw01 = keep.tile([P, PACK, BANK], F32, name="w1_01", tag="raw", bufs=2, align_bytes=64)
        rows01 = w1[PASS : 2 * PASS, 0:PASS].rearrange("(p j) c -> p j c", j=PACK)
        for half in range(2):
            cols = slice(256 * half, 256 * (half + 1))
            nc.sync.dma_start(out=raw01[:, :, cols], in_=rows01[:, :, cols])
        place_scale_rows(v_planes, v_rows, 5, 4 * K_PASSES)

        def first_stage(b, stationary):
            tiles = []
            for t in range(PACK):
                h = keep.tile([P, S], F32, name="h_%d%d" % (b, t), tag="h_%d%d" % (b, t), align_bytes=64)
                accs = [bank(2 * (t % 2) + half, "acc_%d%d%d" % (b, t, half)) for half in range(S // BANK)]
                for a in range(K_PASSES):
                    codes, scales = stationary(t, a)
                    for half, acc in enumerate(accs):
                        cols = slice(BANK * half, BANK * (half + 1))
                        nc.tensor.matmul_mx(
                            out=acc[:],
                            lhsT=codes.bitcast(FP8X4),
                            lhsT_scale=scales,
                            rhs=v_words[a][:, cols].bitcast(FP4X4),
                            rhs_scale=v_planes[a][:, cols],
                            start=(a == 0),
                            stop=(a == K_PASSES - 1),
                        )
                for half, acc in enumerate(accs):
                    nc.scalar.activation(
                        out=h[:, BANK * half : BANK * (half + 1)],
                        in_=acc[:],
                        func=ACT.Abs,
                        bias=bias_t[:, b, t : t + 1],
                        scale=gain_t[:, b, t : t + 1],
                    )
                tiles.append(h)
            return tiles

        def pick(b, hs, m0, m1, tag):
            g1 = keep.tile([P, PACK, m1 - m0], F32, name="g1_%d_%d" % (b, m0), tag=tag + "1")
            g2 = keep.tile([P, PACK, m1 - m0], F32, name="g2_%d_%d" % (b, m0), tag=tag + "2")
            for t in range(PACK):
                nc.vector.tensor_copy(out=g1[:, t, :], in_=hs[t][:].indirect(pos1_t[:, m0 // 16 : m1 // 16]))
                nc.vector.tensor_copy(out=g2[:, t, :], in_=hs[t][:].indirect(pos2_t[:, m0 // 16 : m1 // 16]))
            return g1, g2

        def stronger(grouped, g1, g2):
            nc.vector.tensor_tensor(
                out=grouped.rearrange("p (c i t) -> p c t i", i=2, t=PACK),
                in0=g1[:].rearrange("p t (c i) -> p c t i", i=2),
                in1=g2[:].rearrange("p t (c i) -> p c t i", i=2),
                op=ALU.max,
            )

        def mx_tiles(name, shape):
            codes = keep.tile(shape, U32, name=name + "_codes", align_bytes=64)
            scales = keep.tile(shape, U8, name=name + "_scales", align_bytes=64)
            return codes, scales

        def turn_sens(j0, j1):
            turned = []
            for j in range(j0, j1):
                st = keep.tile([P, N_GROUPS, PACK, P], F32, name="sens_turned%d" % j)
                for g in range(N_GROUPS):
                    acc = bank(4 + (N_GROUPS * j + g) % 4, "sens_acc%d%d" % (j, g))
                    for t in range(PACK):
                        nc.tensor.transpose(acc[:, P * t : P * (t + 1)], sens_t[g][:, t, P * j : P * (j + 1)], ident[:])
                    nc.scalar.copy(out=st[:, g].rearrange("p t q -> p (t q)"), in_=acc[:])
                turned.append(st)
            return turned

        def load_w2_scales():
            planes = keep.tile([P, H_PASSES, N], U8, name="w2_planes", tag="h_03", align_bytes=64)
            nc.gpsimd.memset(planes[:].rearrange("p a c -> p (a c)").bitcast(I32), 0)
            for q in range(4):
                nc.sync.dma_start(
                    out=planes[32 * q : 32 * q + 4].bitcast(I32),
                    in_=w2_scales[:, 4 * q : 4 * q + 4, :].rearrange("a r c -> r a c").bitcast(I32),
                )
            return planes

        def load_sens(g, tag):
            rows = keep.tile([P, PACK, M], F32, name="sens%d" % g, tag=tag, align_bytes=64)
            nc.sync.dma_start(out=rows[:], in_=sens[PASS * g : PASS * (g + 1), :].rearrange("(p t) m -> p t m", t=PACK))
            return rows

        def quantize_into(tiles, grouped, c0, c1):
            codes, scales = tiles
            nc.vector.quantize_mx(
                out=codes[:, c0:c1].bitcast(FP8X4), scales=scales[:, c0:c1], in_=grouped[:, PACK * c0 : PACK * c1]
            )

        def later_weights(b):
            grouped = keep.tile([P, K_PASSES * PACK * BANK], BF16, name="w1g_%d" % b, tag="weights%d" % b, align_bytes=64)
            dealt = grouped[:].rearrange("p (t a q j) -> p a q j t", t=PACK, a=K_PASSES, j=PACK)
            for a in range(K_PASSES):
                raw = load_w1(b, a)
                nc.scalar.copy(out=dealt[:, a], in_=raw[:].rearrange("p j (q t) -> p q j t", t=PACK))
            tiles = mx_tiles("w1_%d" % b, [P, K_PASSES * BANK])
            for c0, c1 in ((0, 256), (256, 512), (512, 1024)):
                quantize_into(tiles, grouped, c0, c1)

            def columns(t, a):
                cols = slice(P * (K_PASSES * t + a), P * (K_PASSES * t + a + 1))
                return tiles[0][:, cols], tiles[1][:, cols]

            return columns

        grouped00 = grouped_tile("w1g_00", "grouped0")
        grouped01 = grouped_tile("w1g_01", "grouped1")
        w1q = [mx_tiles("w1_0%d" % a, [P, BANK]) for a in range(K_PASSES)]
        cast_w1(nc.scalar.copy, grouped00, raw00, 0, P, 0, 1)
        quantize_into(w1q[0], grouped00, 0, P)
        for half in range(2):
            cast_w1(nc.vector.tensor_copy, grouped01, raw01, 64 * half, 64 * (half + 1), 0, 1)
        quantize_into(w1q[1], grouped01, 0, P)
        cast_w1(nc.scalar.copy, grouped00, raw00, 0, P, 1, PACK)
        cast_w1(nc.scalar.copy, grouped01, raw01, 0, 64, 1, PACK)
        cast_w1(nc.vector.tensor_copy, grouped01, raw01, 64, P, 1, PACK)
        for a, grouped in enumerate((grouped00, grouped01)):
            quantize_into(w1q[a], grouped, P, 2 * P)
            quantize_into(w1q[a], grouped, 2 * P, BANK)
        stationary = lambda t, a: (w1q[a][0][:, P * t : P * (t + 1)], w1q[a][1][:, P * t : P * (t + 1)])
        ident = keep.tile([P, P], F32, name="ident")
        make_identity(nc, ident[:])
        hs = first_stage(0, stationary)
        xq = []
        for b in range(H_PASSES - 1):
            g1, g2 = pick(b, hs, 0, M, "g")
            stationary = later_weights(b + 1)
            if b == 1:
                sens_turned = turn_sens(0, 2)
            hs = first_stage(b + 1, stationary)
            if b == 1:
                sens_turned = sens_turned + turn_sens(2, 4)
            if b == 0:
                sens_t = [load_sens(g, "h_0%d" % (2 * g)) for g in range(N_GROUPS)]
                w2_t = keep.tile([P, H_PASSES, N], U16, name="w2_t", tag="h_01", align_bytes=64)
                nc.sync.dma_start(out=w2_t[:].bitcast(I32), in_=w2_words.rearrange("a p c -> p a c").bitcast(I32))
                w2_planes = load_w2_scales()
            grouped = grouped_tile("xg_%d" % b, "weights%d" % (b + 1))
            stronger(grouped[:], g1, g2)
            xq.append(quantize("x%d" % b, grouped))

        last = H_PASSES - 1
        x_codes, x_scales = mx_tiles("x_last", [P, M])
        xq.append((x_codes, x_scales))
        y_codes, y_scales = mx_tiles("y", [P, N_GROUPS, M])
        ys = [keep.tile([P, PACK, M], F32, name="y%d" % g) for g in range(N_GROUPS)]

        def sums_out(j, add_here):
            m = slice(P * j, P * (j + 1))
            sums = [bank(2 * (j % 2) + g, "sum%d%d" % (j, g)) for g in range(N_GROUPS)]
            for b in range(H_PASSES):
                codes, scales = xq[b]
                for g in range(N_GROUPS):
                    n = slice(PASS * g, PASS * (g + 1))
                    nc.tensor.matmul_mx(
                        out=sums[g][:],
                        lhsT=codes[:, m].bitcast(FP8X4),
                        lhsT_scale=scales[:, m],
                        rhs=w2_t[:, b, n].bitcast(FP4X4),
                        rhs_scale=w2_planes[:, b, n],
                        start=(b == 0),
                        stop=(b == H_PASSES - 1),
                    )
            zs = []
            for g in range(N_GROUPS):
                z = keep.tile([P, PACK, P], F32, name="z%d%d" % (j, g), tag="z%d" % g, bufs=2)
                dealt = sums[g][:].rearrange("p (q t) -> p t q", t=PACK)
                if add_here:
                    nc.vector.tensor_tensor(out=z[:], in0=dealt, in1=sens_turned[j][:, g], op=ALU.add)
                else:
                    nc.scalar.copy(out=z[:], in_=dealt)
                zs.append(z)
            return zs

        def turn_back(j, zs, add_here=True):
            outs = []
            for g in range(N_GROUPS):
                acc = bank(4 + 2 * (j % 2) + g, "y_acc%d%d" % (j, g))
                sources = (sens_turned[j][:, g], zs[g][:]) if add_here else (zs[g][:],)
                for i, source in enumerate(sources):
                    for t in range(PACK):
                        nc.tensor.matmul(
                            out=acc[:, P * t : P * (t + 1)],
                            lhsT=source[:, t, :],
                            rhs=ident[:],
                            is_transpose=True,
                            start=(i == 0 and t == 0),
                            stop=(i == len(sources) - 1 and t == PACK - 1),
                        )
                outs.append(acc)
            return outs

        def make_planes(j, outs, copies):
            m = slice(P * j, P * (j + 1))
            for g in range(N_GROUPS):
                woven = keep.tile([P, PACK * P], BF16, name="yg%d%d" % (j, g), tag="yg%d%d" % (j, g), align_bytes=64)
                copies[g](
                    out=woven[:].rearrange("p (m t) -> p m t", t=PACK),
                    in_=outs[g][:].rearrange("p (t m) -> p m t", t=PACK),
                )
                nc.vector.quantize_mx(out=y_codes[:, g, m].bitcast(FP8X4), scales=y_scales[:, g, m], in_=woven[:])

        def keep_scores(j, outs, copies):
            for g in range(N_GROUPS):
                copies[g](out=ys[g][:, :, P * j : P * (j + 1)], in_=outs[g][:].rearrange("p (t m) -> p t m", t=PACK))

        def store(m0, m1):
            for g in range(N_GROUPS):
                rows = out_0[PASS * g : PASS * (g + 1), :].rearrange("(p t) m -> p t m", t=PACK)
                nc.sync.dma_start(out=rows[:, :, m0:m1], in_=ys[g][:, :, m0:m1])
            nc.sync.dma_start(
                out=out_1[:, :, m0:m1, :].rearrange("g p m t -> p g (m t)").bitcast(I32),
                in_=y_codes[:, :, m0:m1].bitcast(I32),
            )

        def last_block(m0, m1, tag, grouped_tag):
            g1, g2 = pick(last, hs, m0, m1, tag)
            grouped = keep.tile([P, PACK * (m1 - m0)], BF16, name="xg_last%d" % m0, tag=grouped_tag, align_bytes=64)
            stronger(grouped[:], g1, g2)
            nc.vector.quantize_mx(out=x_codes[:, m0:m1].bitcast(FP8X4), scales=x_scales[:, m0:m1], in_=grouped[:])

        on_scalar = (nc.scalar.copy, nc.scalar.copy)
        shared = (nc.vector.tensor_copy, nc.scalar.copy)
        last_block(0, 256, "g", "xg_a")
        zs = [sums_out(j, False) for j in range(2)]
        outs0 = turn_back(0, zs[0])
        make_planes(0, outs0, on_scalar)
        keep_scores(0, outs0, on_scalar)
        outs1 = turn_back(1, zs[1])
        make_planes(1, outs1, on_scalar)
        last_block(256, 384, "g", "xg_b")
        zs2 = sums_out(2, False)
        keep_scores(1, outs1, on_scalar)
        store(0, 256)
        outs2 = turn_back(2, zs2)
        make_planes(2, outs2, on_scalar)
        keep_scores(2, outs2, on_scalar)
        store(256, 384)
        last_block(384, 512, "g", "yg11")
        outs3 = turn_back(3, sums_out(3, True), False)
        make_planes(3, outs3, shared)
        keep_scores(3, outs3, shared)
        store(384, 512)
        for q in range(4):
            queue = nc.scalar if q % 2 else nc.sync
            queue.dma_start(
                out=out_2[:, 4 * q : 4 * q + 4, :].rearrange("g r m -> r g m").bitcast(I32),
                in_=y_scales[32 * q : 32 * q + 4].bitcast(I32),
            )
